import numpy as np
import ml_dtypes


def mxq(x, axis, fmt="e4m3"):
    dtype, down = {"e4m3": (ml_dtypes.float8_e4m3fn, 7), "e5m2": (ml_dtypes.float8_e5m2, 14)}[fmt]
    v = np.moveaxis(np.asarray(x, np.float32).astype(ml_dtypes.bfloat16).astype(np.float64), axis, -1)
    blocks = v.reshape(v.shape[:-1] + (-1, 32))
    amax = np.abs(blocks).max(-1, keepdims=True)
    byte = np.maximum(np.where(amax > 0, np.frexp(amax)[1] - 1 + 127, 0) - down, 1)
    scale = np.exp2(byte - 127.0)
    codes = (blocks / scale).astype(np.float32).astype(dtype).astype(np.float64)
    return np.moveaxis((codes * scale).reshape(v.shape), -1, axis)


WIDE = False


def mx_kscale(k):
    if not WIDE:
        return np.ones(k)
    levels = np.array([10, -10, 5, -5, 0])
    if k % 512:
        return np.exp2(np.random.permutation(np.resize(levels, k // 32))).repeat(32)
    a = np.empty((k // 512, 16))
    for p in range(k // 512):
        a[p, :8] = np.random.permutation(np.resize(levels, 8))
        for g in range(8):
            far = levels[np.abs(levels - a[p, g]) >= 10]
            a[p, g + 8] = far[np.random.randint(len(far))]
    return np.exp2(a.ravel()).repeat(32)


def f64(x):
    return np.asarray(x).astype(np.float64)


def striped(idx):
    return np.tile(idx.reshape(-1, 16).T, (8, 1)).astype(np.uint16)


def unstriped(offs):
    return offs[:16].T.reshape(-1).astype(np.int64)


E2M1 = np.array([0.0, 0.5, 1.0, 1.5, 2.0, 3.0, 4.0, 6.0, -0.0, -0.5, -1.0, -1.5, -2.0, -3.0, -4.0, -6.0])


def pack_fp4(w):
    k, n = w.shape
    w = f64(np.asarray(w, np.float32).astype(ml_dtypes.bfloat16)).reshape(k // 32, 32, n)
    amax = np.abs(w).max(1)
    mant, ex = np.frexp(amax / 6.0)
    byte = np.clip(np.where(amax > 0, np.where(mant > 0.5, ex, ex - 1) + 127, 1), 1, 254)
    scaled = (w * np.exp2(127.0 - byte)[:, None, :]).reshape(k, n).astype(np.float32)
    c = np.ascontiguousarray(scaled.reshape(k // 512, 128, 4, n).transpose(0, 1, 3, 2)).astype(ml_dtypes.float4_e2m1fn).view(np.uint8) & 0xF
    words = (c[..., 0::2] | (c[..., 1::2] << 4)).reshape(k // 512, 128, 2 * n)
    return np.ascontiguousarray(words), np.ascontiguousarray(byte.astype(np.uint8).reshape(k // 512, 16, n))


def unpack_fp4(words, scales):
    g, _, n = scales.shape
    words = np.ascontiguousarray(words).reshape(g, 128, n, 2)
    nib = np.empty((g, 128, n, 4), np.uint8)
    nib[..., 0::2] = words & 0xF
    nib[..., 1::2] = words >> 4
    vals = E2M1[nib] * np.repeat(np.exp2(scales.astype(np.float64) - 127.0), 8, axis=1)[..., None]
    return vals.transpose(0, 1, 3, 2).reshape(g * 512, n)


K, T, S, V, H, N = 1024, 1024, 768, 256, 512, 128


def setup_inputs():
    n = np.random.standard_normal
    s = mx_kscale(K)[:, None]
    u = mx_kscale(H)
    packed_w4 = pack_fp4(n((H, N)) / np.sqrt(H) / u[:, None])
    return {
        "xT": (n((K, T)) * s).astype(np.float32),
        "w1": (n((K, H)) / np.sqrt(K) / s * u).astype(np.float32),
        "w2": (n((K, H)) / np.sqrt(K) / s).astype(np.float32),
        "w3": (n((K, H)) / np.sqrt(K) / s).astype(np.float32),
        "w4_words": packed_w4[0],
        "w4_scales": packed_w4[1],
        "offs": striped(np.random.permutation(T)[:S]),
    }


def reference(xT, w1, w2, w3, w4_words, w4_scales, offs):
    xq = mxq(f64(xT)[:, unstriped(offs)], 0, "e4m3")
    z = (((mxq(f64(w1), 0, "e4m3").T @ xq[:, :V])) * ((mxq(f64(w2), 0, "e4m3").T @ xq[:, V:2 * V]))) * ((mxq(f64(w3), 0, "e4m3").T @ xq[:, 2 * V:3 * V]))
    return unpack_fp4(w4_words, w4_scales).T @ mxq(z, 0, "e4m3")

@@ -1,0 +1,165 @@
+from contextlib import ExitStack
+
+import concourse.mybir as mybir
+from concourse.masks import make_identity
+
+K, T, S, V, H, N = 1024, 1024, 768, 256, 512, 128
+FLOPS = 2 * (3 * K * H * V + H * N * V)
+
+F32 = mybir.dt.float32
+BF16 = mybir.dt.bfloat16
+I32 = mybir.dt.int32
+U32 = mybir.dt.uint32
+U16 = mybir.dt.uint16
+U8 = mybir.dt.uint8
+FP8X4 = mybir.dt.float8_e4m3fn_x4
+FP4X4 = mybir.dt.float4_e2m1fn_x4
+MULT = mybir.AluOpType.mult
+
+P = 128
+PACK = 4
+KP = P * PACK
+PASSES = K // KP
+HALVES = V // P
+X_COLS = 512
+X_VEC = [256,192,128,192]
+W_VEC = [128,128,128,128,128]
+LAST = [[0,256,128],[256,384,64],[384,512,96]]
+
+
+def tile_picked_trilin_none_e_kernel(tc, xT, w1, w2, w3, w4_words, w4_scales, offs, out):
+    nc = tc.nc
+    with ExitStack() as ctx:
+        keep = ctx.enter_context(tc.tile_pool(name="keep", bufs=1))
+        psum = ctx.enter_context(tc.psum_pool(name="psum", bufs=1))
+        banks = [psum.tile([P, 512], F32, name=f"bank{b}") for b in range(8)]
+
+        def load(name, src, g, c0, c1):
+            raw = keep.tile([P, PACK, c1 - c0], F32, name=f"raw_{name}", align_bytes=64)
+            nc.sync.dma_start(out=raw[:], in_=src[g * KP:(g + 1) * KP, c0:c1].rearrange("(p j) c -> p j c", j=PACK))
+            return raw
+
+        def weave(name, raw, on_vector):
+            width = raw.shape[2]
+            grouped = keep.tile([P, width, PACK], BF16, name=f"grouped_{name}", align_bytes=64)
+            for copy, c0, c1 in ((nc.scalar.copy, on_vector, width), (nc.vector.tensor_copy, 0, on_vector)):
+                if c1 > c0:
+                    copy(out=grouped[:, c0:c1, :].rearrange("p (c i) j -> p c j i", i=4),
+                         in_=raw[:, :, c0:c1].rearrange("p j (c i) -> p c j i", i=4))
+            return grouped
+
+        def quantize(grouped, words, scales):
+            nc.vector.quantize_mx(out=words.bitcast(FP8X4), scales=scales, in_=grouped[:].rearrange("p c j -> p (c j)"))
+
+        x_scales = keep.tile([P, T], U8, name="x_scales", align_bytes=64)
+        nc.gpsimd.memset(x_scales[:], 0)
+        w4_plane = keep.tile([P, N], U8, name="w4_plane", align_bytes=64)
+        nc.gpsimd.memset(w4_plane[:], 0)
+        ident = keep.tile([P, P], F32, name="ident", align_bytes=64)
+        make_identity(nc, ident[:])
+
+        offsets = keep.tile([P, S // 16], U16, name="offsets")
+        x_raw = []
+        for g in range(PASSES):
+            for c0 in range(0, T, X_COLS):
+                x_raw.append((g, c0, load(f"x{g}_{c0}", xT, g, c0, c0 + X_COLS)))
+                if len(x_raw) == 1:
+                    nc.sync.dma_start(offsets[:], offs)
+        w_raw = {}
+        for d, w in enumerate((w1, w2)):
+            for g in range(PASSES):
+                w_raw[d, g] = load(f"w{d}_{g}", w, g, 0, H)
+        w4_codes = keep.tile([P, 2 * N], U8, name="w4_codes", align_bytes=64)
+        nc.sync.dma_start(out=w4_codes[:].bitcast(I32), in_=w4_words[0].bitcast(I32))
+        for q in range(4):
+            nc.sync.dma_start(out=w4_plane[32 * q:32 * q + 4, :].bitcast(I32), in_=w4_scales[0, 4 * q:4 * q + 4, :].bitcast(I32))
+        w_raw[2, 0] = load("w2_0", w3, 0, 0, H)
+        last_raw = [load(f"w2_1_{c0}", w3, 1, c0, c1) for c0, c1, vec in LAST]
+
+        x_words = [keep.tile([P, T], U32, name=f"x_words{g}", align_bytes=64) for g in range(PASSES)]
+        picked_words = {}
+        picked_scales = {}
+
+        def gather_words(g, d):
+            picked_words[g, d] = keep.tile([P, V], U32, name=f"picked_words{g}_{d}", align_bytes=64)
+            nc.vector.tensor_copy(out=picked_words[g, d][:], in_=x_words[g][:].indirect(offsets[:, d * (V // 16):(d + 1) * (V // 16)]))
+
+        def gather_scales(d):
+            picked_scales[d] = keep.tile([P, V], U8, name=f"picked_scales{d}", align_bytes=64)
+            nc.vector.tensor_copy(out=picked_scales[d][:], in_=x_scales[:].indirect(offsets[:, d * (V // 16):(d + 1) * (V // 16)]))
+
+        for n, (g, c0, raw) in enumerate(x_raw):
+            grouped = weave(f"x{g}_{c0}", raw, X_VEC[n])
+            for q0 in range(0, X_COLS, 512):
+                nc.vector.quantize_mx(out=x_words[g][:, c0 + q0:c0 + q0 + 512].bitcast(FP8X4),
+                                      scales=x_scales[4 * g:P, c0 + q0:c0 + q0 + 512],
+                                      in_=grouped[:, q0:q0 + 512, :].rearrange("p c j -> p (c j)"))
+            if g == 0 and c0 + X_COLS == T:
+                for d in range(3):
+                    gather_words(0, d)
+
+        def quantize_weights(name, raw, on_vector):
+            width = raw.shape[2]
+            grouped = weave(name, raw, on_vector)
+            words = keep.tile([P, width], U32, name=f"words_{name}", align_bytes=64)
+            scales = keep.tile([P, width], U8, name=f"scales_{name}", align_bytes=64)
+            quantize(grouped, words[:], scales[:])
+            return words, scales
+
+        def product(acc, d, g, h, words, scales):
+            cols = slice(h * P, (h + 1) * P)
+            nc.tensor.matmul_mx(out=acc, lhsT=picked_words[g, d][:, cols].bitcast(FP8X4), lhsT_scale=picked_scales[d][4 * g:P, cols],
+                                rhs=words.bitcast(FP8X4), rhs_scale=scales, start=(g == 0), stop=(g == PASSES - 1))
+
+        def paired(ap):
+            return ap.rearrange("p (m u e) -> p u m e", u=2, e=2)
+
+        first = [keep.tile([P, 2, P, 2], F32, name=f"first{h}", align_bytes=64) for h in range(HALVES)]
+        both = [keep.tile([P, 2, P, 2], F32, name=f"both{h}", align_bytes=64) for h in range(HALVES)]
+        z = [keep.tile([P, 2, P, 2], BF16, name=f"z{h}", align_bytes=64) for h in range(HALVES)]
+
+        for d in range(2):
+            gather_words(1, d)
+            gather_scales(d)
+            for g in range(PASSES):
+                words, scales = quantize_weights(f"w{d}_{g}", w_raw[d, g], W_VEC[2 * d + g])
+                for h in range(HALVES):
+                    product(banks[2 * d + h][:], d, g, h, words[:], scales[:])
+            for h in range(HALVES):
+                if d == 0:
+                    nc.scalar.copy(out=first[h][:], in_=paired(banks[h][:]))
+                else:
+                    nc.vector.tensor_tensor(out=both[h][:], in0=paired(banks[2 + h][:]), in1=first[h][:], op=MULT)
+        gather_words(1, 2)
+        gather_scales(2)
+        words0, scales0 = quantize_weights("w2_0", w_raw[2, 0], W_VEC[4])
+        last_banks = [(4, 5), (6, 7), (0, 1)]
+        for n, (c0, c1, vec) in enumerate(LAST):
+            for h in range(HALVES):
+                product(banks[last_banks[n][h]][:, 0:c1 - c0], 2, 0, h, words0[:, c0:c1], scales0[:, c0:c1])
+        for n, (c0, c1, vec) in enumerate(LAST):
+            words, scales = quantize_weights(f"w2_1_{c0}", last_raw[n], vec)
+            for h in range(HALVES):
+                acc = banks[last_banks[n][h]][:, 0:c1 - c0]
+                product(acc, 2, 1, h, words[:], scales[:])
+                nc.vector.tensor_tensor(out=z[h][:, :, c0 // 4:c1 // 4, :], in0=paired(acc), in1=both[h][:, :, c0 // 4:c1 // 4, :], op=MULT)
+
+        result = keep.tile([P, V], F32, name="result", align_bytes=64)
+        for h in range(HALVES):
+            turned = banks[2 + h]
+            for u in range(2):
+                nc.tensor.transpose(turned[:, u * P:(u + 1) * P], z[h][:, u, :, :].rearrange("p m e -> p (m e)").bitcast(F32), ident[:])
+            z_grouped = keep.tile([P, P, PACK], BF16, name=f"z_grouped{h}", align_bytes=64)
+            nc.scalar.copy(out=z_grouped[:].rearrange("p v j -> p (v j)").bitcast(F32).rearrange("p (v u) -> p v u", u=2),
+                           in_=turned[:, 0:2 * P].rearrange("p (u v) -> p v u", u=2))
+            z_words = keep.tile([P, P], U32, name=f"z_words{h}", align_bytes=64)
+            z_scales = keep.tile([P, P], U8, name=f"z_scales{h}", align_bytes=64)
+            quantize(z_grouped, z_words[:], z_scales[:])
+            acc = banks[4 + h][:, 0:P]
+            nc.tensor.matmul_mx(out=acc, lhsT=w4_codes[:].bitcast(FP4X4), lhsT_scale=w4_plane[:],
+                                rhs=z_words[:].bitcast(FP8X4), rhs_scale=z_scales[:], start=True, stop=True)
+            if h == 0:
+                nc.scalar.copy(out=result[:, 0:P], in_=acc)
+            else:
+                nc.vector.tensor_copy(out=result[:, P:V], in_=acc)
+        nc.sync.dma_start(out=out, in_=result[:])

@@ -21,10 +21,15 @@ PACK = 4
 KP = P * PACK
 PASSES = K // KP
 HALVES = V // P
-X_COLS = 512
-X_VEC = [256,192,128,192]
-W_VEC = [128,128,128,128,128]
-LAST = [[0,256,128],[256,384,64],[384,512,96]]
+LOADS = [('x', 0, 0, 1024, [(512, 384), (512, 256)]), ('x', 1, 0, 1024, [(512, 256), (512, 352)]), ('a', 0, 0, 512, [(512, 64)]), ('a', 1, 0, 512, [(512, 0)]), ('b', 0, 0, 512, [(512, 192)]), ('b', 1, 0, 512, [(512, 192)]), ('c', 0, 0, 512, [(256, 192), (256, 64)]), ('c', 1, 0, 512, [(256, 64), (256, 128)])]
+OFFS_AFTER = 0
+W4_AFTER = 5
+GATHERS = {('x', 0): [(0, 0), (0, 2), (0, 1)], ('x', 1): [(1, 0), (2, 0), (2, 1), (1, 1)], ('a', 1, 0): [], ('a', 0, 0): [(2, 2)], ('b', 0, 0): [(1, 2)], ('b', 1, 0): []}
+HOLD = {(1, 2): 'grouped_b0_0', (2, 2): 'raw_a0_0'}
+GROUPS = [[(0, 512, (0, 1))], [(0, 512, (2, 3))], [(0, 256, (4, 5)), (256, 512, (6, 7))]]
+FIRST_ON_VECTOR = [False, False]
+TURN_BANKS = (0, 1)
+OUT_BANKS = (4, 5)
 
 
 def tile_picked_trilin_none_e_kernel(tc, xT, w1, w2, w3, w4_words, w4_scales, offs, out):
@@ -59,52 +64,29 @@ def tile_picked_trilin_none_e_kernel(tc, xT, w1, w2, w3, w4_words, w4_scales, of
         make_identity(nc, ident[:])
 
         offsets = keep.tile([P, S // 16], U16, name="offsets")
-        x_raw = []
-        for g in range(PASSES):
-            for c0 in range(0, T, X_COLS):
-                x_raw.append((g, c0, load(f"x{g}_{c0}", xT, g, c0, c0 + X_COLS)))
-                if len(x_raw) == 1:
-                    nc.sync.dma_start(offsets[:], offs)
-        w_raw = {}
-        for d, w in enumerate((w1, w2)):
-            for g in range(PASSES):
-                w_raw[d, g] = load(f"w{d}_{g}", w, g, 0, H)
         w4_codes = keep.tile([P, 2 * N], U8, name="w4_codes", align_bytes=64)
-        nc.sync.dma_start(out=w4_codes[:].bitcast(I32), in_=w4_words[0].bitcast(I32))
-        for q in range(4):
-            nc.sync.dma_start(out=w4_plane[32 * q:32 * q + 4, :].bitcast(I32), in_=w4_scales[0, 4 * q:4 * q + 4, :].bitcast(I32))
-        w_raw[2, 0] = load("w2_0", w3, 0, 0, H)
-        last_raw = [load(f"w2_1_{c0}", w3, 1, c0, c1) for c0, c1, vec in LAST]
+        sources = {"x": xT, "a": w1, "b": w2, "c": w3}
+        raws = []
+        for n, (key, g, c0, c1, blocks) in enumerate(LOADS):
+            raws.append(load(f"{key}{g}_{c0}", sources[key], g, c0, c1))
+            if n == OFFS_AFTER:
+                nc.sync.dma_start(offsets[:], offs)
+            if n == W4_AFTER:
+                nc.sync.dma_start(out=w4_codes[:].bitcast(I32), in_=w4_words[0].bitcast(I32))
+                for q in range(4):
+                    nc.sync.dma_start(out=w4_plane[32 * q:32 * q + 4, :].bitcast(I32), in_=w4_scales[0, 4 * q:4 * q + 4, :].bitcast(I32))
 
         x_words = [keep.tile([P, T], U32, name=f"x_words{g}", align_bytes=64) for g in range(PASSES)]
         picked_words = {}
         picked_scales = {}
 
         def gather_words(g, d):
-            picked_words[g, d] = keep.tile([P, V], U32, name=f"picked_words{g}_{d}", align_bytes=64)
+            picked_words[g, d] = keep.tile([P, V], U32, name=f"picked_words{g}_{d}", tag=HOLD.get((g, d), f"picked_words{g}_{d}"), align_bytes=64)
             nc.vector.tensor_copy(out=picked_words[g, d][:], in_=x_words[g][:].indirect(offsets[:, d * (V // 16):(d + 1) * (V // 16)]))
 
         def gather_scales(d):
-            picked_scales[d] = keep.tile([P, V], U8, name=f"picked_scales{d}", align_bytes=64)
+            picked_scales[d] = keep.tile([P, V], U8, name=f"picked_scales{d}", tag=HOLD.get((2, d), f"picked_scales{d}"), align_bytes=64)
             nc.vector.tensor_copy(out=picked_scales[d][:], in_=x_scales[:].indirect(offsets[:, d * (V // 16):(d + 1) * (V // 16)]))
-
-        for n, (g, c0, raw) in enumerate(x_raw):
-            grouped = weave(f"x{g}_{c0}", raw, X_VEC[n])
-            for q0 in range(0, X_COLS, 512):
-                nc.vector.quantize_mx(out=x_words[g][:, c0 + q0:c0 + q0 + 512].bitcast(FP8X4),
-                                      scales=x_scales[4 * g:P, c0 + q0:c0 + q0 + 512],
-                                      in_=grouped[:, q0:q0 + 512, :].rearrange("p c j -> p (c j)"))
-            if g == 0 and c0 + X_COLS == T:
-                for d in range(3):
-                    gather_words(0, d)
-
-        def quantize_weights(name, raw, on_vector):
-            width = raw.shape[2]
-            grouped = weave(name, raw, on_vector)
-            words = keep.tile([P, width], U32, name=f"words_{name}", align_bytes=64)
-            scales = keep.tile([P, width], U8, name=f"scales_{name}", align_bytes=64)
-            quantize(grouped, words[:], scales[:])
-            return words, scales
 
         def product(acc, d, g, h, words, scales):
             cols = slice(h * P, (h + 1) * P)
@@ -117,36 +99,50 @@ def tile_picked_trilin_none_e_kernel(tc, xT, w1, w2, w3, w4_words, w4_scales, of
         first = [keep.tile([P, 2, P, 2], F32, name=f"first{h}", align_bytes=64) for h in range(HALVES)]
         both = [keep.tile([P, 2, P, 2], F32, name=f"both{h}", align_bytes=64) for h in range(HALVES)]
         z = [keep.tile([P, 2, P, 2], BF16, name=f"z{h}", align_bytes=64) for h in range(HALVES)]
-
-        for d in range(2):
-            gather_words(1, d)
-            gather_scales(d)
-            for g in range(PASSES):
-                words, scales = quantize_weights(f"w{d}_{g}", w_raw[d, g], W_VEC[2 * d + g])
-                for h in range(HALVES):
-                    product(banks[2 * d + h][:], d, g, h, words[:], scales[:])
-            for h in range(HALVES):
-                if d == 0:
-                    nc.scalar.copy(out=first[h][:], in_=paired(banks[h][:]))
+        w_words = {}
+        w_scales = {}
+        for n, (key, g, c0, c1, blocks) in enumerate(LOADS):
+            d = "abcx".index(key)
+            if d < 3 and (d, g) not in w_words:
+                w_words[d, g] = keep.tile([P, H], U32, name=f"words_{key}{g}", align_bytes=64)
+                w_scales[d, g] = keep.tile([P, H], U8, name=f"scales_{key}{g}", align_bytes=64)
+            b0 = c0
+            for width, on_vector in blocks:
+                b1 = b0 + width
+                grouped = weave(f"{key}{g}_{b0}", raws[n][:, :, b0 - c0:b1 - c0], on_vector)
+                if key == "x":
+                    quantize(grouped, x_words[g][:, b0:b1], x_scales[4 * g:P, b0:b1])
                 else:
-                    nc.vector.tensor_tensor(out=both[h][:], in0=paired(banks[2 + h][:]), in1=first[h][:], op=MULT)
-        gather_words(1, 2)
-        gather_scales(2)
-        words0, scales0 = quantize_weights("w2_0", w_raw[2, 0], W_VEC[4])
-        last_banks = [(4, 5), (6, 7), (0, 1)]
-        for n, (c0, c1, vec) in enumerate(LAST):
-            for h in range(HALVES):
-                product(banks[last_banks[n][h]][:, 0:c1 - c0], 2, 0, h, words0[:, c0:c1], scales0[:, c0:c1])
-        for n, (c0, c1, vec) in enumerate(LAST):
-            words, scales = quantize_weights(f"w2_1_{c0}", last_raw[n], vec)
-            for h in range(HALVES):
-                acc = banks[last_banks[n][h]][:, 0:c1 - c0]
-                product(acc, 2, 1, h, words[:], scales[:])
-                nc.vector.tensor_tensor(out=z[h][:, :, c0 // 4:c1 // 4, :], in0=paired(acc), in1=both[h][:, :, c0 // 4:c1 // 4, :], op=MULT)
+                    quantize(grouped, w_words[d, g][:, b0:b1], w_scales[d, g][:, b0:b1])
+                    for item in GATHERS.get((key, g, b0), []):
+                        if item[0] == 2:
+                            gather_scales(item[1])
+                        else:
+                            gather_words(item[0], item[1])
+                    for g0, g1, pair in GROUPS[d]:
+                        if b0 < g1 <= b1:
+                            for h in range(HALVES):
+                                acc = banks[pair[h]][:, 0:g1 - g0]
+                                product(acc, d, g, h, w_words[d, g][:, g0:g1], w_scales[d, g][:, g0:g1])
+                                if g == PASSES - 1:
+                                    m = slice(g0 // 4, g1 // 4)
+                                    if d == 0:
+                                        (nc.vector.tensor_copy if FIRST_ON_VECTOR[h] else nc.scalar.copy)(out=first[h][:, :, m, :], in_=paired(acc))
+                                    elif d == 1:
+                                        nc.vector.tensor_tensor(out=both[h][:, :, m, :], in0=paired(acc), in1=first[h][:, :, m, :], op=MULT)
+                                    else:
+                                        nc.vector.tensor_tensor(out=z[h][:, :, m, :], in0=paired(acc), in1=both[h][:, :, m, :], op=MULT)
+                b0 = b1
+                if key == "x" and b1 == T:
+                    for item in GATHERS[key, g]:
+                        if item[0] == 2:
+                            gather_scales(item[1])
+                        else:
+                            gather_words(item[0], item[1])
 
         result = keep.tile([P, V], F32, name="result", align_bytes=64)
         for h in range(HALVES):
-            turned = banks[2 + h]
+            turned = banks[TURN_BANKS[h]]
             for u in range(2):
                 nc.tensor.transpose(turned[:, u * P:(u + 1) * P], z[h][:, u, :, :].rearrange("p m e -> p (m e)").bitcast(F32), ident[:])
             z_grouped = keep.tile([P, P, PACK], BF16, name=f"z_grouped{h}", align_bytes=64)
@@ -155,7 +151,7 @@ def tile_picked_trilin_none_e_kernel(tc, xT, w1, w2, w3, w4_words, w4_scales, of
             z_words = keep.tile([P, P], U32, name=f"z_words{h}", align_bytes=64)
             z_scales = keep.tile([P, P], U8, name=f"z_scales{h}", align_bytes=64)
             quantize(z_grouped, z_words[:], z_scales[:])
-            acc = banks[4 + h][:, 0:P]
+            acc = banks[OUT_BANKS[h]][:, 0:P]
             nc.tensor.matmul_mx(out=acc, lhsT=w4_codes[:].bitcast(FP4X4), lhsT_scale=w4_plane[:],
                                 rhs=z_words[:].bitcast(FP8X4), rhs_scale=z_scales[:], start=True, stop=True)
             if h == 0:

@@ -21,11 +21,11 @@ PACK = 4
 KP = P * PACK
 PASSES = K // KP
 HALVES = V // P
-LOADS = [('x', 0, 0, 1024, [(512, 384), (512, 256)]), ('x', 1, 0, 1024, [(512, 256), (512, 352)]), ('a', 0, 0, 512, [(512, 64)]), ('a', 1, 0, 512, [(512, 0)]), ('b', 0, 0, 512, [(512, 192)]), ('b', 1, 0, 512, [(512, 192)]), ('c', 0, 0, 512, [(256, 192), (256, 64)]), ('c', 1, 0, 512, [(256, 64), (256, 128)])]
+LOADS = [('x', 0, 0, 512, [(512, 288)]), ('x', 0, 512, 1024, [(256, 96), (256, 192)]), ('x', 1, 0, 512, [(256, 64), (256, 96)]), ('x', 1, 512, 1024, [(256, 64), (128, 96), (128, 32)]), ('a', 0, 0, 512, [(512, 128)]), ('a', 1, 0, 512, [(512, 0)]), ('b', 0, 0, 512, [(512, 320)]), ('b', 1, 0, 512, [(512, 288)]), ('c', 0, 0, 512, [(256, 192), (256, 96)]), ('c', 1, 0, 256, [(256, 0)]), ('c', 1, 256, 512, [(128, 32), (128, 64)])]
 OFFS_AFTER = 0
-W4_AFTER = 5
-GATHERS = {('x', 0): [(0, 0), (0, 2), (0, 1)], ('x', 1): [(1, 0), (2, 0), (2, 1), (1, 1)], ('a', 1, 0): [], ('a', 0, 0): [(2, 2)], ('b', 0, 0): [(1, 2)], ('b', 1, 0): []}
-HOLD = {(1, 2): 'grouped_b0_0', (2, 2): 'raw_a0_0'}
+W4_AFTER = 10
+GATHERS = {('x', 0): [(0, 0), (0, 2), (0, 1)], ('x', 1): [(1, 0), (2, 0), (2, 2)], ('b', 0, 0): [(1, 2)], ('a', 1, 0): [], ('a', 0, 0): [(1, 1), (2, 1)], ('b', 1, 0): []}
+HOLD = {(1, 1): 'raw_a0_0', (2, 1): 'grouped_a0_0', (1, 2): 'grouped_b0_0'}
 GROUPS = [[(0, 512, (0, 1))], [(0, 512, (2, 3))], [(0, 256, (4, 5)), (256, 512, (6, 7))]]
 FIRST_ON_VECTOR = [False, False]
 TURN_BANKS = (0, 1)
@@ -49,8 +49,8 @@ def tile_picked_trilin_none_e_kernel(tc, xT, w1, w2, w3, w4_words, w4_scales, of
             grouped = keep.tile([P, width, PACK], BF16, name=f"grouped_{name}", align_bytes=64)
             for copy, c0, c1 in ((nc.scalar.copy, on_vector, width), (nc.vector.tensor_copy, 0, on_vector)):
                 if c1 > c0:
-                    copy(out=grouped[:, c0:c1, :].rearrange("p (c i) j -> p c j i", i=4),
-                         in_=raw[:, :, c0:c1].rearrange("p j (c i) -> p c j i", i=4))
+                    copy(out=grouped[:, c0:c1, :].rearrange("p (c i) j -> p c j i", i=2),
+                         in_=raw[:, :, c0:c1].rearrange("p j (c i) -> p c j i", i=2))
             return grouped
 
         def quantize(grouped, words, scales):
@@ -101,8 +101,33 @@ def tile_picked_trilin_none_e_kernel(tc, xT, w1, w2, w3, w4_words, w4_scales, of
         z = [keep.tile([P, 2, P, 2], BF16, name=f"z{h}", align_bytes=64) for h in range(HALVES)]
         w_words = {}
         w_scales = {}
+
+        def gathers(items):
+            for item in items:
+                if item[0] == 2:
+                    gather_scales(item[1])
+                else:
+                    gather_words(item[0], item[1])
+
+        def products(d, g, b0, b1):
+            for g0, g1, pair in GROUPS[d]:
+                if b0 < g1 <= b1:
+                    for h in range(HALVES):
+                        acc = banks[pair[h]][:, 0:g1 - g0]
+                        product(acc, d, g, h, w_words[d, g][:, g0:g1], w_scales[d, g][:, g0:g1])
+                        if g == PASSES - 1:
+                            m = slice(g0 // 4, g1 // 4)
+                            if d == 0:
+                                (nc.vector.tensor_copy if FIRST_ON_VECTOR[h] else nc.scalar.copy)(out=first[h][:, :, m, :], in_=paired(acc))
+                            elif d == 1:
+                                nc.vector.tensor_tensor(out=both[h][:, :, m, :], in0=paired(acc), in1=first[h][:, :, m, :], op=MULT)
+                            else:
+                                nc.vector.tensor_tensor(out=z[h][:, :, m, :], in0=paired(acc), in1=both[h][:, :, m, :], op=MULT)
+
+        waiting = []
+        entities_ready = False
         for n, (key, g, c0, c1, blocks) in enumerate(LOADS):
-            d = "abcx".index(key)
+            d = ["a", "b", "c", "x"].index(key)
             if d < 3 and (d, g) not in w_words:
                 w_words[d, g] = keep.tile([P, H], U32, name=f"words_{key}{g}", align_bytes=64)
                 w_scales[d, g] = keep.tile([P, H], U8, name=f"scales_{key}{g}", align_bytes=64)
@@ -112,33 +137,20 @@ def tile_picked_trilin_none_e_kernel(tc, xT, w1, w2, w3, w4_words, w4_scales, of
                 grouped = weave(f"{key}{g}_{b0}", raws[n][:, :, b0 - c0:b1 - c0], on_vector)
                 if key == "x":
                     quantize(grouped, x_words[g][:, b0:b1], x_scales[4 * g:P, b0:b1])
+                    if b1 == T:
+                        gathers(GATHERS[key, g])
+                        if g == PASSES - 1:
+                            entities_ready = True
+                            for item in waiting:
+                                products(*item)
                 else:
                     quantize(grouped, w_words[d, g][:, b0:b1], w_scales[d, g][:, b0:b1])
-                    for item in GATHERS.get((key, g, b0), []):
-                        if item[0] == 2:
-                            gather_scales(item[1])
-                        else:
-                            gather_words(item[0], item[1])
-                    for g0, g1, pair in GROUPS[d]:
-                        if b0 < g1 <= b1:
-                            for h in range(HALVES):
-                                acc = banks[pair[h]][:, 0:g1 - g0]
-                                product(acc, d, g, h, w_words[d, g][:, g0:g1], w_scales[d, g][:, g0:g1])
-                                if g == PASSES - 1:
-                                    m = slice(g0 // 4, g1 // 4)
-                                    if d == 0:
-                                        (nc.vector.tensor_copy if FIRST_ON_VECTOR[h] else nc.scalar.copy)(out=first[h][:, :, m, :], in_=paired(acc))
-                                    elif d == 1:
-                                        nc.vector.tensor_tensor(out=both[h][:, :, m, :], in0=paired(acc), in1=first[h][:, :, m, :], op=MULT)
-                                    else:
-                                        nc.vector.tensor_tensor(out=z[h][:, :, m, :], in0=paired(acc), in1=both[h][:, :, m, :], op=MULT)
+                    gathers(GATHERS.get((key, g, b0), []))
+                    if entities_ready:
+                        products(d, g, b0, b1)
+                    else:
+                        waiting.append((d, g, b0, b1))
                 b0 = b1
-                if key == "x" and b1 == T:
-                    for item in GATHERS[key, g]:
-                        if item[0] == 2:
-                            gather_scales(item[1])
-                        else:
-                            gather_words(item[0], item[1])
 
         result = keep.tile([P, V], F32, name="result", align_bytes=64)
         for h in range(HALVES):

@@ -21,15 +21,16 @@ PACK = 4
 KP = P * PACK
 PASSES = K // KP
 HALVES = V // P
-LOADS = [('x', 0, 0, 512, [(512, 288)]), ('x', 0, 512, 1024, [(256, 96), (256, 192)]), ('x', 1, 0, 512, [(256, 64), (256, 96)]), ('x', 1, 512, 1024, [(256, 64), (128, 96), (128, 32)]), ('a', 0, 0, 512, [(512, 128)]), ('a', 1, 0, 512, [(512, 0)]), ('b', 0, 0, 512, [(512, 320)]), ('b', 1, 0, 512, [(512, 288)]), ('c', 0, 0, 512, [(256, 192), (256, 96)]), ('c', 1, 0, 256, [(256, 0)]), ('c', 1, 256, 512, [(128, 32), (128, 64)])]
+LOADS = [('x', 0, 0, 1024, [(256, 224), (256, 160), (512, 224)]), ('x', 1, 0, 1024, [(512, 224), (512, 416)]), ('a', 0, 0, 512, [(512, 0)]), ('a', 1, 0, 512, [(512, 128)]), ('b', 0, 0, 512, [(512, 160)]), ('b', 1, 0, 512, [(256, 256), (256, 96)]), ('c', 0, 0, 512, [(128, 32), (128, 0), (256, 224)]), ('c', 1, 0, 512, [(256, 128), (256, 160)])]
 OFFS_AFTER = 0
-W4_AFTER = 10
-GATHERS = {('x', 0): [(0, 0), (0, 2), (0, 1)], ('x', 1): [(1, 0), (2, 0), (2, 2)], ('b', 0, 0): [(1, 2)], ('a', 1, 0): [], ('a', 0, 0): [(1, 1), (2, 1)], ('b', 1, 0): []}
-HOLD = {(1, 1): 'raw_a0_0', (2, 1): 'grouped_a0_0', (1, 2): 'grouped_b0_0'}
+W4_AFTER = 7
+GATHERS = {'now': [(3, 0), (3, 1)], ('x', 0): [(0, 0), (0, 2)], ('x', 1): [(1, 0), (2, 0), (2, 2), (1, 1)], ('b', 0, 0): [(2, 1)], ('a', 1, 0): [(0, 1)], ('b', 1, 0): [], ('c', 0, 128): [(4, 0)], ('a', 0, 0): [(1, 2)], ('c', 0, 256): [], ('c', 1, 0): [(4, 1)], ('b', 1, 256): []}
+HOLD = {(4, 1): 'grouped_c1_0', (1, 2): 'grouped_a0_0', (4, 0): 'grouped_c0_128', (0, 1): 'grouped_a1_0', (2, 1): 'raw_b0_0'}
 GROUPS = [[(0, 512, (0, 1))], [(0, 512, (2, 3))], [(0, 256, (4, 5)), (256, 512, (6, 7))]]
 FIRST_ON_VECTOR = [False, False]
 TURN_BANKS = (0, 1)
 OUT_BANKS = (4, 5)
+EARLY = {}
 
 
 def tile_picked_trilin_none_e_kernel(tc, xT, w1, w2, w3, w4_words, w4_scales, offs, out):
@@ -49,9 +50,16 @@ def tile_picked_trilin_none_e_kernel(tc, xT, w1, w2, w3, w4_words, w4_scales, of
             grouped = keep.tile([P, width, PACK], BF16, name=f"grouped_{name}", align_bytes=64)
             for copy, c0, c1 in ((nc.scalar.copy, on_vector, width), (nc.vector.tensor_copy, 0, on_vector)):
                 if c1 > c0:
-                    copy(out=grouped[:, c0:c1, :].rearrange("p (c i) j -> p c j i", i=2),
-                         in_=raw[:, :, c0:c1].rearrange("p j (c i) -> p c j i", i=2))
+                    copy(out=grouped[:, c0:c1, :].rearrange("p (c i) j -> p c j i", i=4),
+                         in_=raw[:, :, c0:c1].rearrange("p j (c i) -> p c j i", i=4))
             return grouped
+
+        def weave_pair(grouped, raw, u, on_vector):
+            width = raw.shape[2]
+            for copy, c0, c1 in ((nc.scalar.copy, on_vector, width), (nc.vector.tensor_copy, 0, on_vector)):
+                if c1 > c0:
+                    copy(out=grouped[:, c0:c1, 2 * u:2 * u + 2].rearrange("p (c i) j -> p c j i", i=4),
+                         in_=raw[:, :, c0:c1].rearrange("p j (c i) -> p c j i", i=4))
 
         def quantize(grouped, words, scales):
             nc.vector.quantize_mx(out=words.bitcast(FP8X4), scales=scales, in_=grouped[:].rearrange("p c j -> p (c j)"))
@@ -68,7 +76,16 @@ def tile_picked_trilin_none_e_kernel(tc, xT, w1, w2, w3, w4_words, w4_scales, of
         sources = {"x": xT, "a": w1, "b": w2, "c": w3}
         raws = []
         for n, (key, g, c0, c1, blocks) in enumerate(LOADS):
-            raws.append(load(f"{key}{g}_{c0}", sources[key], g, c0, c1))
+            if key == "x" and g in EARLY:
+                rows = xT[g * KP:(g + 1) * KP, :].rearrange("(p j) c -> p j c", j=PACK)
+                pair = []
+                for u in range(2):
+                    half = keep.tile([P, 2, T], F32, name=f"raw_x{g}_pair{u}", align_bytes=64)
+                    nc.sync.dma_start(out=half[:], in_=rows[:, 2 * u:2 * u + 2, :])
+                    pair.append(half)
+                raws.append(pair)
+            else:
+                raws.append(load(f"{key}{g}_{c0}", sources[key], g, c0, c1))
             if n == OFFS_AFTER:
                 nc.sync.dma_start(offsets[:], offs)
             if n == W4_AFTER:
@@ -96,8 +113,8 @@ def tile_picked_trilin_none_e_kernel(tc, xT, w1, w2, w3, w4_words, w4_scales, of
         def paired(ap):
             return ap.rearrange("p (m u e) -> p u m e", u=2, e=2)
 
-        first = [keep.tile([P, 2, P, 2], F32, name=f"first{h}", align_bytes=64) for h in range(HALVES)]
-        both = [keep.tile([P, 2, P, 2], F32, name=f"both{h}", align_bytes=64) for h in range(HALVES)]
+        first = {}
+        both = {}
         z = [keep.tile([P, 2, P, 2], BF16, name=f"z{h}", align_bytes=64) for h in range(HALVES)]
         w_words = {}
         w_scales = {}
@@ -106,6 +123,14 @@ def tile_picked_trilin_none_e_kernel(tc, xT, w1, w2, w3, w4_words, w4_scales, of
             for item in items:
                 if item[0] == 2:
                     gather_scales(item[1])
+                elif item[0] == 3:
+                    h = item[1]
+                    first[h] = keep.tile([P, 2, P, 2], F32, name=f"first{h}", tag=HOLD.get(item, f"first{h}"), align_bytes=64)
+                    (nc.vector.tensor_copy if FIRST_ON_VECTOR[h] else nc.scalar.copy)(out=first[h][:], in_=paired(banks[h][:]))
+                elif item[0] == 4:
+                    h = item[1]
+                    both[h] = keep.tile([P, 2, P, 2], F32, name=f"both{h}", tag=HOLD.get(item, f"both{h}"), align_bytes=64)
+                    nc.vector.tensor_tensor(out=both[h][:], in0=paired(banks[2 + h][:]), in1=first[h][:], op=MULT)
                 else:
                     gather_words(item[0], item[1])
 
@@ -117,10 +142,8 @@ def tile_picked_trilin_none_e_kernel(tc, xT, w1, w2, w3, w4_words, w4_scales, of
                         product(acc, d, g, h, w_words[d, g][:, g0:g1], w_scales[d, g][:, g0:g1])
                         if g == PASSES - 1:
                             m = slice(g0 // 4, g1 // 4)
-                            if d == 0:
-                                (nc.vector.tensor_copy if FIRST_ON_VECTOR[h] else nc.scalar.copy)(out=first[h][:, :, m, :], in_=paired(acc))
-                            elif d == 1:
-                                nc.vector.tensor_tensor(out=both[h][:, :, m, :], in0=paired(acc), in1=first[h][:, :, m, :], op=MULT)
+                            if d < 2:
+                                gathers([item for item in GATHERS["now"] if item == (3 + d, h)])
                             else:
                                 nc.vector.tensor_tensor(out=z[h][:, :, m, :], in0=paired(acc), in1=both[h][:, :, m, :], op=MULT)
 
@@ -132,9 +155,20 @@ def tile_picked_trilin_none_e_kernel(tc, xT, w1, w2, w3, w4_words, w4_scales, of
                 w_words[d, g] = keep.tile([P, H], U32, name=f"words_{key}{g}", align_bytes=64)
                 w_scales[d, g] = keep.tile([P, H], U8, name=f"scales_{key}{g}", align_bytes=64)
             b0 = c0
+            early = {}
+            if key == "x" and g in EARLY:
+                for width, on_vector in blocks:
+                    early[b0] = keep.tile([P, width, PACK], BF16, name=f"grouped_x{g}_{b0}", align_bytes=64)
+                    weave_pair(early[b0], raws[n][0][:, :, b0:b0 + width], 0, EARLY[g] * width // 256 * 32)
+                    b0 = b0 + width
+            b0 = c0
             for width, on_vector in blocks:
                 b1 = b0 + width
-                grouped = weave(f"{key}{g}_{b0}", raws[n][:, :, b0 - c0:b1 - c0], on_vector)
+                if early:
+                    grouped = early[b0]
+                    weave_pair(grouped, raws[n][1][:, :, b0:b1], 1, on_vector)
+                else:
+                    grouped = weave(f"{key}{g}_{b0}", raws[n][:, :, b0 - c0:b1 - c0], on_vector)
                 if key == "x":
                     quantize(grouped, x_words[g][:, b0:b1], x_scales[4 * g:P, b0:b1])
                     if b1 == T:
@@ -170,4 +204,4 @@ def tile_picked_trilin_none_e_kernel(tc, xT, w1, w2, w3, w4_words, w4_scales, of
                 nc.scalar.copy(out=result[:, 0:P], in_=acc)
             else:
                 nc.vector.tensor_copy(out=result[:, P:V], in_=acc)
-        nc.sync.dma_start(out=out, in_=result[:])
+            nc.sync.dma_start(out=out[:, h * P:(h + 1) * P], in_=result[:, h * P:(h + 1) * P])

from contextlib import ExitStack

import concourse.mybir as mybir
from concourse.masks import make_identity

K, T, S, V, H, N = 1024, 1024, 768, 256, 512, 128
FLOPS = 2 * (3 * K * H * V + H * N * V)

F32 = mybir.dt.float32
BF16 = mybir.dt.bfloat16
I32 = mybir.dt.int32
U32 = mybir.dt.uint32
U16 = mybir.dt.uint16
U8 = mybir.dt.uint8
FP8X4 = mybir.dt.float8_e4m3fn_x4
FP4X4 = mybir.dt.float4_e2m1fn_x4
MULT = mybir.AluOpType.mult

P = 128
PACK = 4
KP = P * PACK
PASSES = K // KP
HALVES = V // P
LOADS = [('x', 0, 0, 1024, [(256, 224), (256, 160), (512, 224)]), ('x', 1, 0, 1024, [(512, 224), (512, 416)]), ('a', 0, 0, 512, [(512, 0)]), ('a', 1, 0, 512, [(512, 128)]), ('b', 0, 0, 512, [(512, 160)]), ('b', 1, 0, 512, [(256, 256), (256, 96)]), ('c', 0, 0, 512, [(128, 32), (128, 0), (256, 224)]), ('c', 1, 0, 512, [(256, 128), (256, 160)])]
OFFS_AFTER = 0
W4_AFTER = 7
GATHERS = {'now': [(3, 0), (3, 1)], ('x', 0): [(0, 0), (0, 2)], ('x', 1): [(1, 0), (2, 0), (2, 2), (1, 1)], ('b', 0, 0): [(2, 1)], ('a', 1, 0): [(0, 1)], ('b', 1, 0): [], ('c', 0, 128): [(4, 0)], ('a', 0, 0): [(1, 2)], ('c', 0, 256): [], ('c', 1, 0): [(4, 1)], ('b', 1, 256): []}
HOLD = {(4, 1): 'grouped_c1_0', (1, 2): 'grouped_a0_0', (4, 0): 'grouped_c0_128', (0, 1): 'grouped_a1_0', (2, 1): 'raw_b0_0'}
GROUPS = [[(0, 512, (0, 1))], [(0, 512, (2, 3))], [(0, 256, (4, 5)), (256, 512, (6, 7))]]
FIRST_ON_VECTOR = [False, False]
TURN_BANKS = (0, 1)
OUT_BANKS = (4, 5)
EARLY = {}


def tile_picked_trilin_none_e_kernel(tc, xT, w1, w2, w3, w4_words, w4_scales, offs, out):
    nc = tc.nc
    with ExitStack() as ctx:
        keep = ctx.enter_context(tc.tile_pool(name="keep", bufs=1))
        psum = ctx.enter_context(tc.psum_pool(name="psum", bufs=1))
        banks = [psum.tile([P, 512], F32, name=f"bank{b}") for b in range(8)]

        def load(name, src, g, c0, c1):
            raw = keep.tile([P, PACK, c1 - c0], F32, name=f"raw_{name}", align_bytes=64)
            nc.sync.dma_start(out=raw[:], in_=src[g * KP:(g + 1) * KP, c0:c1].rearrange("(p j) c -> p j c", j=PACK))
            return raw

        def weave(name, raw, on_vector):
            width = raw.shape[2]
            grouped = keep.tile([P, width, PACK], BF16, name=f"grouped_{name}", align_bytes=64)
            for copy, c0, c1 in ((nc.scalar.copy, on_vector, width), (nc.vector.tensor_copy, 0, on_vector)):
                if c1 > c0:
                    copy(out=grouped[:, c0:c1, :].rearrange("p (c i) j -> p c j i", i=4),
                         in_=raw[:, :, c0:c1].rearrange("p j (c i) -> p c j i", i=4))
            return grouped

        def weave_pair(grouped, raw, u, on_vector):
            width = raw.shape[2]
            for copy, c0, c1 in ((nc.scalar.copy, on_vector, width), (nc.vector.tensor_copy, 0, on_vector)):
                if c1 > c0:
                    copy(out=grouped[:, c0:c1, 2 * u:2 * u + 2].rearrange("p (c i) j -> p c j i", i=4),
                         in_=raw[:, :, c0:c1].rearrange("p j (c i) -> p c j i", i=4))

        def quantize(grouped, words, scales):
            nc.vector.quantize_mx(out=words.bitcast(FP8X4), scales=scales, in_=grouped[:].rearrange("p c j -> p (c j)"))

        x_scales = keep.tile([P, T], U8, name="x_scales", align_bytes=64)
        nc.gpsimd.memset(x_scales[:], 0)
        w4_plane = keep.tile([P, N], U8, name="w4_plane", align_bytes=64)
        nc.gpsimd.memset(w4_plane[:], 0)
        ident = keep.tile([P, P], F32, name="ident", align_bytes=64)
        make_identity(nc, ident[:])

        offsets = keep.tile([P, S // 16], U16, name="offsets")
        w4_codes = keep.tile([P, 2 * N], U8, name="w4_codes", align_bytes=64)
        sources = {"x": xT, "a": w1, "b": w2, "c": w3}
        raws = []
        for n, (key, g, c0, c1, blocks) in enumerate(LOADS):
            if key == "x" and g in EARLY:
                rows = xT[g * KP:(g + 1) * KP, :].rearrange("(p j) c -> p j c", j=PACK)
                pair = []
                for u in range(2):
                    half = keep.tile([P, 2, T], F32, name=f"raw_x{g}_pair{u}", align_bytes=64)
                    nc.sync.dma_start(out=half[:], in_=rows[:, 2 * u:2 * u + 2, :])
                    pair.append(half)
                raws.append(pair)
            else:
                raws.append(load(f"{key}{g}_{c0}", sources[key], g, c0, c1))
            if n == OFFS_AFTER:
                nc.sync.dma_start(offsets[:], offs)
            if n == W4_AFTER:
                nc.sync.dma_start(out=w4_codes[:].bitcast(I32), in_=w4_words[0].bitcast(I32))
                for q in range(4):
                    nc.sync.dma_start(out=w4_plane[32 * q:32 * q + 4, :].bitcast(I32), in_=w4_scales[0, 4 * q:4 * q + 4, :].bitcast(I32))

        x_words = [keep.tile([P, T], U32, name=f"x_words{g}", align_bytes=64) for g in range(PASSES)]
        picked_words = {}
        picked_scales = {}

        def gather_words(g, d):
            picked_words[g, d] = keep.tile([P, V], U32, name=f"picked_words{g}_{d}", tag=HOLD.get((g, d), f"picked_words{g}_{d}"), align_bytes=64)
            nc.vector.tensor_copy(out=picked_words[g, d][:], in_=x_words[g][:].indirect(offsets[:, d * (V // 16):(d + 1) * (V // 16)]))

        def gather_scales(d):
            picked_scales[d] = keep.tile([P, V], U8, name=f"picked_scales{d}", tag=HOLD.get((2, d), f"picked_scales{d}"), align_bytes=64)
            nc.vector.tensor_copy(out=picked_scales[d][:], in_=x_scales[:].indirect(offsets[:, d * (V // 16):(d + 1) * (V // 16)]))

        def product(acc, d, g, h, words, scales):
            cols = slice(h * P, (h + 1) * P)
            nc.tensor.matmul_mx(out=acc, lhsT=picked_words[g, d][:, cols].bitcast(FP8X4), lhsT_scale=picked_scales[d][4 * g:P, cols],
                                rhs=words.bitcast(FP8X4), rhs_scale=scales, start=(g == 0), stop=(g == PASSES - 1))

        def paired(ap):
            return ap.rearrange("p (m u e) -> p u m e", u=2, e=2)

        first = {}
        both = {}
        z = [keep.tile([P, 2, P, 2], BF16, name=f"z{h}", align_bytes=64) for h in range(HALVES)]
        w_words = {}
        w_scales = {}

        def gathers(items):
            for item in items:
                if item[0] == 2:
                    gather_scales(item[1])
                elif item[0] == 3:
                    h = item[1]
                    first[h] = keep.tile([P, 2, P, 2], F32, name=f"first{h}", tag=HOLD.get(item, f"first{h}"), align_bytes=64)
                    (nc.vector.tensor_copy if FIRST_ON_VECTOR[h] else nc.scalar.copy)(out=first[h][:], in_=paired(banks[h][:]))
                elif item[0] == 4:
                    h = item[1]
                    both[h] = keep.tile([P, 2, P, 2], F32, name=f"both{h}", tag=HOLD.get(item, f"both{h}"), align_bytes=64)
                    nc.vector.tensor_tensor(out=both[h][:], in0=paired(banks[2 + h][:]), in1=first[h][:], op=MULT)
                else:
                    gather_words(item[0], item[1])

        def products(d, g, b0, b1):
            for g0, g1, pair in GROUPS[d]:
                if b0 < g1 <= b1:
                    for h in range(HALVES):
                        acc = banks[pair[h]][:, 0:g1 - g0]
                        product(acc, d, g, h, w_words[d, g][:, g0:g1], w_scales[d, g][:, g0:g1])
                        if g == PASSES - 1:
                            m = slice(g0 // 4, g1 // 4)
                            if d < 2:
                                gathers([item for item in GATHERS["now"] if item == (3 + d, h)])
                            else:
                                nc.vector.tensor_tensor(out=z[h][:, :, m, :], in0=paired(acc), in1=both[h][:, :, m, :], op=MULT)

        waiting = []
        entities_ready = False
        for n, (key, g, c0, c1, blocks) in enumerate(LOADS):
            d = ["a", "b", "c", "x"].index(key)
            if d < 3 and (d, g) not in w_words:
                w_words[d, g] = keep.tile([P, H], U32, name=f"words_{key}{g}", align_bytes=64)
                w_scales[d, g] = keep.tile([P, H], U8, name=f"scales_{key}{g}", align_bytes=64)
            b0 = c0
            early = {}
            if key == "x" and g in EARLY:
                for width, on_vector in blocks:
                    early[b0] = keep.tile([P, width, PACK], BF16, name=f"grouped_x{g}_{b0}", align_bytes=64)
                    weave_pair(early[b0], raws[n][0][:, :, b0:b0 + width], 0, EARLY[g] * width // 256 * 32)
                    b0 = b0 + width
            b0 = c0
            for width, on_vector in blocks:
                b1 = b0 + width
                if early:
                    grouped = early[b0]
                    weave_pair(grouped, raws[n][1][:, :, b0:b1], 1, on_vector)
                else:
                    grouped = weave(f"{key}{g}_{b0}", raws[n][:, :, b0 - c0:b1 - c0], on_vector)
                if key == "x":
                    quantize(grouped, x_words[g][:, b0:b1], x_scales[4 * g:P, b0:b1])
                    if b1 == T:
                        gathers(GATHERS[key, g])
                        if g == PASSES - 1:
                            entities_ready = True
                            for item in waiting:
                                products(*item)
                else:
                    quantize(grouped, w_words[d, g][:, b0:b1], w_scales[d, g][:, b0:b1])
                    gathers(GATHERS.get((key, g, b0), []))
                    if entities_ready:
                        products(d, g, b0, b1)
                    else:
                        waiting.append((d, g, b0, b1))
                b0 = b1

        result = keep.tile([P, V], F32, name="result", align_bytes=64)
        for h in range(HALVES):
            turned = banks[TURN_BANKS[h]]
            for u in range(2):
                nc.tensor.transpose(turned[:, u * P:(u + 1) * P], z[h][:, u, :, :].rearrange("p m e -> p (m e)").bitcast(F32), ident[:])
            z_grouped = keep.tile([P, P, PACK], BF16, name=f"z_grouped{h}", align_bytes=64)
            nc.scalar.copy(out=z_grouped[:].rearrange("p v j -> p (v j)").bitcast(F32).rearrange("p (v u) -> p v u", u=2),
                           in_=turned[:, 0:2 * P].rearrange("p (u v) -> p v u", u=2))
            z_words = keep.tile([P, P], U32, name=f"z_words{h}", align_bytes=64)
            z_scales = keep.tile([P, P], U8, name=f"z_scales{h}", align_bytes=64)
            quantize(z_grouped, z_words[:], z_scales[:])
            acc = banks[OUT_BANKS[h]][:, 0:P]
            nc.tensor.matmul_mx(out=acc, lhsT=w4_codes[:].bitcast(FP4X4), lhsT_scale=w4_plane[:],
                                rhs=z_words[:].bitcast(FP8X4), rhs_scale=z_scales[:], start=True, stop=True)
            if h == 0:
                nc.scalar.copy(out=result[:, 0:P], in_=acc)
            else:
                nc.vector.tensor_copy(out=result[:, P:V], in_=acc)
            nc.sync.dma_start(out=out[:, h * P:(h + 1) * P], in_=result[:, h * P:(h + 1) * P])
